import numpy as np
import ml_dtypes


def mxq(x, axis, fmt="e4m3"):
    dtype, down = {"e4m3": (ml_dtypes.float8_e4m3fn, 7), "e5m2": (ml_dtypes.float8_e5m2, 14)}[fmt]
    v = np.moveaxis(np.asarray(x, np.float32).astype(ml_dtypes.bfloat16).astype(np.float64), axis, -1)
    blocks = v.reshape(v.shape[:-1] + (-1, 32))
    amax = np.abs(blocks).max(-1, keepdims=True)
    byte = np.maximum(np.where(amax > 0, np.frexp(amax)[1] - 1 + 127, 0) - down, 1)
    scale = np.exp2(byte - 127.0)
    codes = (blocks / scale).astype(np.float32).astype(dtype).astype(np.float64)
    return np.moveaxis((codes * scale).reshape(v.shape), -1, axis)


WIDE = False


def mx_kscale(k):
    if not WIDE:
        return np.ones(k)
    levels = np.array([10, -10, 5, -5, 0])
    if k % 512:
        return np.exp2(np.random.permutation(np.resize(levels, k // 32))).repeat(32)
    a = np.empty((k // 512, 16))
    for p in range(k // 512):
        a[p, :8] = np.random.permutation(np.resize(levels, 8))
        for g in range(8):
            far = levels[np.abs(levels - a[p, g]) >= 10]
            a[p, g + 8] = far[np.random.randint(len(far))]
    return np.exp2(a.ravel()).repeat(32)


def f64(x):
    return np.asarray(x).astype(np.float64)


def striped(idx):
    return np.tile(idx.reshape(-1, 16).T, (8, 1)).astype(np.uint16)


def unstriped(offs):
    return offs[:16].T.reshape(-1).astype(np.int64)


E2M1 = np.array([0.0, 0.5, 1.0, 1.5, 2.0, 3.0, 4.0, 6.0, -0.0, -0.5, -1.0, -1.5, -2.0, -3.0, -4.0, -6.0])


def pack_fp4(w):
    k, n = w.shape
    w = f64(np.asarray(w, np.float32).astype(ml_dtypes.bfloat16)).reshape(k // 32, 32, n)
    amax = np.abs(w).max(1)
    mant, ex = np.frexp(amax / 6.0)
    byte = np.clip(np.where(amax > 0, np.where(mant > 0.5, ex, ex - 1) + 127, 1), 1, 254)
    scaled = (w * np.exp2(127.0 - byte)[:, None, :]).reshape(k, n).astype(np.float32)
    c = np.ascontiguousarray(scaled.reshape(k // 512, 128, 4, n).transpose(0, 1, 3, 2)).astype(ml_dtypes.float4_e2m1fn).view(np.uint8) & 0xF
    words = (c[..., 0::2] | (c[..., 1::2] << 4)).reshape(k // 512, 128, 2 * n)
    return np.ascontiguousarray(words), np.ascontiguousarray(byte.astype(np.uint8).reshape(k // 512, 16, n))


def unpack_fp4(words, scales):
    g, _, n = scales.shape
    words = np.ascontiguousarray(words).reshape(g, 128, n, 2)
    nib = np.empty((g, 128, n, 4), np.uint8)
    nib[..., 0::2] = words & 0xF
    nib[..., 1::2] = words >> 4
    vals = E2M1[nib] * np.repeat(np.exp2(scales.astype(np.float64) - 127.0), 8, axis=1)[..., None]
    return vals.transpose(0, 1, 3, 2).reshape(g * 512, n)


def relu(v):
    return np.maximum(v, 0.0)


K, T, S, D, V, H, N, U = 512, 2048, 512, 3, 512, 512, 256, 1024
P = 2 ** 7


def setup_inputs():
    n = np.random.standard_normal
    s = mx_kscale(K)[:, None]
    u = mx_kscale(H)
    packed_w2 = pack_fp4(n((H, N)) / np.sqrt(H) / u[:, None])
    return {
        "xT": (n((K, T)) * s).astype(np.float32),
        "w1": (n((K, H)) / np.sqrt(K) / s * u).astype(np.float32),
        "w2_words": packed_w2[0],
        "w2_scales": packed_w2[1],
        "gate": np.tile(np.random.uniform(0.2, 0.6, (D, 1, V)), (1, P, 1)).astype(np.float32),
        "emb": (0.5 * n((H, U)) * u[:, None]).astype(np.float32),
        "offs": striped(np.random.permutation(T)[:S]),
        "cell": striped(np.random.permutation(U)[:S]),
        "pos1": striped(np.random.permutation(U)[:V]),
        "pos2": striped(np.random.permutation(U)[:V]),
        "pos3": striped(np.random.permutation(U)[:V]),
    }


def reference(xT, w1, w2_words, w2_scales, gate, emb, offs, cell, pos1, pos2, pos3):
    xq = mxq(f64(xT)[:, unstriped(offs)], 0, "e4m3")
    up = np.zeros((H, U))
    up[:, unstriped(cell)] = relu(mxq(f64(w1), 0, "e4m3").T @ xq)
    z = up + f64(emb)
    y = unpack_fp4(w2_words, w2_scales).T @ mxq(z, 0, "e4m3")
    return y[:, unstriped(pos1)] * f64(gate)[0, :1] + y[:, unstriped(pos2)] * f64(gate)[1, :1] + y[:, unstriped(pos3)] * f64(gate)[2, :1]

@@ -1,0 +1,235 @@
+from contextlib import ExitStack
+
+import concourse.mybir as mybir
+from concourse.masks import make_identity
+
+K, T, S, V, H, N, U = 512, 2048, 512, 512, 512, 256, 1024
+FLOPS = 2 * K * H * S + 2 * H * N * U
+
+F32 = mybir.dt.float32
+BF16 = mybir.dt.bfloat16
+I32 = mybir.dt.int32
+U32 = mybir.dt.uint32
+U16 = mybir.dt.uint16
+U8 = mybir.dt.uint8
+FP8X4 = mybir.dt.float8_e4m3fn_x4
+FP4X4 = mybir.dt.float4_e2m1fn_x4
+ADD = mybir.AluOpType.add
+MULT = mybir.AluOpType.mult
+COPY = mybir.ActivationFunctionType.Copy
+RELU = mybir.ActivationFunctionType.Relu
+
+P = 128
+PACK = 4
+HALF = S // 2
+PIECE = 256
+LIST = 16
+
+
+def tile_picked_devox_none_e_kernel(
+    tc, xT, w1, w2_words, w2_scales, gate, emb, offs, cell, pos1, pos2, pos3, out
+):
+    nc = tc.nc
+    with ExitStack() as ctx:
+        lists = ctx.enter_context(tc.tile_pool(name="lists", bufs=1))
+        sb = ctx.enter_context(tc.tile_pool(name="sb", bufs=1))
+        psum = ctx.enter_context(tc.psum_pool(name="psum", bufs=1))
+
+        def bank(index, shape, dtype, name):
+            return psum.tile(shape, dtype, name=name, tag=f"bank{index}")
+
+        def load_list(source, name):
+            tile = lists.tile([P, S // LIST], U16, name=name)
+            nc.sync.dma_start(tile[:], source)
+            return tile
+
+        def load(source, shape, name):
+            tile = sb.tile(shape, F32, name=name)
+            nc.sync.dma_start(tile[:], source)
+            return tile
+
+        w1_raw = load(w1.rearrange("(p j) c -> p j c", j=PACK), [P, PACK, H], "w1_raw")
+        offs_sb = load_list(offs, "offs_sb")
+        x_rows = xT.rearrange("(p j) c -> j p c", j=PACK)
+        x_plane = [load(x_rows[j], [P, T], f"x_plane{j}") for j in range(PACK)]
+        cell_sb = load_list(cell, "cell_sb")
+        emb_rows = emb.rearrange("(p j) r -> j p r", j=PACK)
+        emb_plane = [load(emb_rows[j], [P, U], f"emb_plane{j}") for j in range(PACK)]
+        gate_sb = [load(gate[d], [P, V], f"gate{d}") for d in range(3)]
+        w2_codes = sb.tile([P, 2 * N], U8, name="w2_codes", align_bytes=64)
+        nc.sync.dma_start(w2_codes[:], w2_words[0])
+        w2_scale = sb.tile([P, N], U8, name="w2_scale", align_bytes=64)
+        nc.vector.memset(w2_scale[:].bitcast(I32), 0)
+        for q in range(4):
+            nc.sync.dma_start(
+                w2_scale[32 * q : 32 * q + 4, :].bitcast(I32),
+                w2_scales[0, 4 * q : 4 * q + 4, :].bitcast(I32),
+            )
+        pos_sb = [load_list(src, f"pos{d}_sb") for d, src in enumerate((pos1, pos2, pos3))]
+
+        ident32 = sb.tile([P, P], F32, name="ident32")
+        make_identity(nc, ident32[:])
+        ident16 = sb.tile([P, P], BF16, name="ident16")
+        make_identity(nc, ident16[:])
+
+        up = [sb.tile([P, U], F32, name=f"up{t}") for t in range(PACK)]
+        for t in range(PACK):
+            nc.vector.memset(up[t][:], 0.0)
+
+        w1_grouped = sb.tile([P, PACK * H], BF16, name="w1_grouped", align_bytes=64)
+        nc.scalar.activation(
+            w1_grouped[:].rearrange("p (t m j) -> p m j t", t=PACK, j=PACK),
+            w1_raw[:].rearrange("p j (m t) -> p m j t", t=PACK),
+            COPY,
+        )
+        w1_codes = sb.tile([P, H], U32, name="w1_codes", align_bytes=64)
+        w1_scale = sb.tile([P, H], U8, name="w1_scale", align_bytes=64)
+        nc.vector.quantize_mx(out=w1_codes[:].bitcast(FP8X4), scales=w1_scale[:], in_=w1_grouped[:])
+
+        x_grouped = [sb.tile([P, HALF, PACK], BF16, name=f"x_grouped{a}", align_bytes=64) for a in range(2)]
+        x_codes = sb.tile([P, S], U32, name="x_codes", align_bytes=64)
+        x_scale = sb.tile([P, S], U8, name="x_scale", align_bytes=64)
+
+        def half_cols(a):
+            return slice(a * HALF, (a + 1) * HALF)
+
+        def half_list(tile, a):
+            return tile[:, a * HALF // LIST : (a + 1) * HALF // LIST]
+
+        for j in range(PACK):
+            for a in range(2):
+                nc.vector.tensor_copy(x_grouped[a][:, :, j], x_plane[j][:].indirect(half_list(offs_sb, a)))
+                if j == PACK - 1:
+                    nc.vector.quantize_mx(
+                        out=x_codes[:, half_cols(a)].bitcast(FP8X4),
+                        scales=x_scale[:, half_cols(a)],
+                        in_=x_grouped[a][:].rearrange("p c j -> p (c j)"),
+                    )
+
+        def first_product(t, cols, bank_index, name):
+            width = cols.stop - cols.start
+            acc = bank(bank_index, [P, width], F32, f"h_acc{name}")
+            m_cols = slice(t * P, (t + 1) * P)
+            nc.tensor.matmul_mx(
+                out=acc[:],
+                lhsT=w1_codes[:, m_cols].bitcast(FP8X4),
+                lhsT_scale=w1_scale[:, m_cols],
+                rhs=x_codes[:, cols].bitcast(FP8X4),
+                rhs_scale=x_scale[:, cols],
+                start=True,
+                stop=True,
+            )
+            h = sb.tile([P, width], F32, name=f"h{name}")
+            nc.scalar.activation(h[:], acc[:], RELU)
+            return h
+
+        h_first = [first_product(0, half_cols(a), a, f"0_{a}") for a in range(2)]
+        h_rest = [first_product(t, slice(0, S), t + 1, f"{t}") for t in range(1, PACK)]
+
+        z_planes = [sb.tile([P, PACK, PIECE], BF16, name=f"z_planes{q}", align_bytes=64) for q in range(U // PIECE)]
+
+        def open_sum(t, banks):
+            sums = []
+            for a in range(2):
+                acc = bank(banks[a], [P, 4, P], F32, f"zT_acc{t}_{a}")
+                for b in range(4):
+                    c0 = (4 * a + b) * P
+                    nc.tensor.matmul(acc[:, b, :], emb_plane[t][:, c0 : c0 + P], ident32[:],
+                                     start=(b == 0), stop=False, is_transpose=True)
+                sums.append(acc)
+            return sums
+
+        def close_sum(t, sums, banks):
+            turned = []
+            for a in range(2):
+                for b in range(4):
+                    c0 = (4 * a + b) * P
+                    nc.tensor.matmul(sums[a][:, b, :], up[t][:, c0 : c0 + P], ident32[:],
+                                     start=False, stop=(b == 3), is_transpose=True)
+                zT = sb.tile([P, 4, P], BF16, name=f"zT{t}_{a}")
+                nc.scalar.copy(zT[:], sums[a][:])
+                turned.append(zT)
+            for a in range(2):
+                back = bank(banks[a], [P, 4, P], BF16, f"z_back{t}_{a}")
+                for b in range(4):
+                    nc.tensor.transpose(back[:, b, :], turned[a][:, b, :], ident16[:])
+                for e in range(2):
+                    nc.scalar.copy(
+                        z_planes[2 * a + e][:, t, :],
+                        back[:, 2 * e : 2 * e + 2, :].rearrange("p b c -> p (b c)"),
+                    )
+
+        sum_banks = [(5, 6), (1, 2), (5, 6)]
+        back_banks = [(7, 0), (3, 4), (7, 0)]
+        for t in range(PACK):
+            if t < PACK - 1:
+                sums = open_sum(t, sum_banks[t])
+            if t == 0:
+                for a in range(2):
+                    nc.vector.tensor_copy(up[0][:].indirect(half_list(cell_sb, a)), h_first[a][:])
+            else:
+                nc.vector.tensor_copy(up[t][:].indirect(cell_sb[:]), h_rest[t - 1][:])
+            if t < PACK - 1:
+                close_sum(t, sums, back_banks[t])
+
+        gate_cols = sb.tile([P, 2, 4], F32, name="gate_cols")
+        for d in range(2):
+            turned = bank(1 + d, [P, 4, P], F32, f"gate_turned{d}")
+            for b in range(4):
+                nc.tensor.transpose(turned[:, b, :], gate_sb[d][:, b * P : (b + 1) * P], ident32[:])
+            nc.scalar.copy(gate_cols[:, d, :], turned[:, :, 0])
+
+        y = [sb.tile([P, U], F32, name=f"y{m}") for m in range(2)]
+        last = PACK - 1
+        for q in range(U // PIECE):
+            cols = slice(q * PIECE, (q + 1) * PIECE)
+            nc.vector.tensor_tensor(z_planes[q][:, last, :], up[last][:, cols], emb_plane[last][:, cols], ADD)
+        z_grouped = [sb.tile([P, PIECE, PACK], BF16, name=f"z_grouped{q}", align_bytes=64) for q in range(U // PIECE)]
+        for q in (0, 2, 1, 3):
+            dst = z_grouped[q][:].rearrange("p (c i) t -> p c t i", i=4)
+            src = z_planes[q][:].rearrange("p t (c i) -> p c t i", i=4)
+            if q % 2 == 0:
+                nc.scalar.copy(dst, src)
+            else:
+                nc.vector.tensor_copy(dst, src)
+        for step, q in enumerate((1, 0, 3, 2)):
+            cols = slice(q * PIECE, (q + 1) * PIECE)
+            z_codes = sb.tile([P, PIECE], U32, name=f"z_codes{q}", align_bytes=64)
+            z_scale = sb.tile([P, PIECE], U8, name=f"z_scale{q}", align_bytes=64)
+            nc.vector.quantize_mx(out=z_codes[:].bitcast(FP8X4), scales=z_scale[:],
+                                  in_=z_grouped[q][:].rearrange("p c t -> p (c t)"))
+            for m in range(2):
+                acc = bank((1 + 2 * step + m) % 8, [P, PIECE], F32, f"y_acc{q}_{m}")
+                nc.tensor.matmul_mx(
+                    out=acc[:],
+                    lhsT=w2_codes[:, 2 * P * m : 2 * P * (m + 1)].bitcast(FP4X4),
+                    lhsT_scale=w2_scale[:, P * m : P * (m + 1)],
+                    rhs=z_codes[:].bitcast(FP8X4),
+                    rhs_scale=z_scale[:],
+                    start=True,
+                    stop=True,
+                )
+                nc.scalar.copy(y[m][:, cols], acc[:])
+
+        partial = []
+        for m in range(2):
+            acc = bank(5 + m, [P, 4, P], F32, f"out_acc{m}")
+            for d in range(2):
+                picked = sb.tile([P, V], F32, name=f"picked{m}_{d}")
+                nc.vector.tensor_copy(picked[:], y[m][:].indirect(pos_sb[d][:]))
+                turned = bank(1 + 2 * m + d, [P, 4, P], F32, f"picked_turned{m}_{d}")
+                for b in range(4):
+                    nc.tensor.transpose(turned[:, b, :], picked[:, b * P : (b + 1) * P], ident32[:])
+                scaled = sb.tile([P, 4, P], F32, name=f"scaled{m}_{d}")
+                for b in range(4):
+                    nc.scalar.activation(scaled[:, b, :], turned[:, b, :], COPY, scale=gate_cols[:, d, b : b + 1])
+                for b in range(4):
+                    nc.tensor.matmul(acc[:, b, :], scaled[:, b, :], ident32[:],
+                                     start=(d == 0 and b == 0), stop=(d == 1 and b == 3), is_transpose=True)
+            partial.append(acc)
+        for m in range(2):
+            third = sb.tile([P, V], F32, name=f"third{m}")
+            nc.vector.tensor_tensor(third[:], y[m][:].indirect(pos_sb[2][:]), gate_sb[2][:], MULT)
+            result = sb.tile([P, V], F32, name=f"result{m}")
+            nc.vector.tensor_tensor(result[:], partial[m][:].rearrange("p b c -> p (b c)"), third[:], ADD)
+            nc.sync.dma_start(out[m * P : (m + 1) * P, :], result[:])

@@ -24,6 +24,7 @@ PACK = 4
 HALF = S // 2
 PIECE = 256
 LIST = 16
+BLOCKS = 4
 
 
 def tile_picked_devox_none_e_kernel(
@@ -48,14 +49,29 @@ def tile_picked_devox_none_e_kernel(
             nc.sync.dma_start(tile[:], source)
             return tile
 
-        w1_raw = load(w1.rearrange("(p j) c -> p j c", j=PACK), [P, PACK, H], "w1_raw")
-        offs_sb = load_list(offs, "offs_sb")
+        def load_emb_rows(tile, h, e):
+            rows = emb.rearrange("(h m t) r -> h t m r", h=2, t=PACK)
+            nc.sync.dma_start(tile[e:P:2, :], rows[h][e])
+
+        w1_halves = w1.rearrange("(p j) (h c) -> h p j c", j=PACK, h=2)
         x_rows = xT.rearrange("(p j) c -> j p c", j=PACK)
-        x_plane = [load(x_rows[j], [P, T], f"x_plane{j}") for j in range(PACK)]
-        cell_sb = load_list(cell, "cell_sb")
         emb_rows = emb.rearrange("(p j) r -> j p r", j=PACK)
-        emb_plane = [load(emb_rows[j], [P, U], f"emb_plane{j}") for j in range(PACK)]
-        gate_sb = [load(gate[d], [P, V], f"gate{d}") for d in range(3)]
+        x_plane = [load(x_rows[0], [P, T], "x_plane0")]
+        offs_sb = load_list(offs, "offs_sb")
+        x_plane.extend(load(x_rows[j], [P, T], f"x_plane{j}") for j in range(1, PACK))
+        w1_low = load(w1_halves[0], [P, PACK, H // 2], "w1_low")
+        cell_sb = load_list(cell, "cell_sb")
+        emb_low = sb.tile([P, U], F32, name="emb_low")
+        load_emb_rows(emb_low, 0, 0)
+        w1_high = sb.tile([P, PACK, H // 2], F32, name="w1_high", tag="w1_high")
+        nc.sync.dma_start(w1_high[:], w1_halves[1])
+        load_emb_rows(emb_low, 0, 1)
+        emb_two = load(emb_rows[2], [P, U], "emb_two")
+        emb_high = sb.tile([P, U], F32, name="emb_high")
+        for e in range(2):
+            load_emb_rows(emb_high, 1, e)
+        emb_three = load(emb_rows[3], [P, U], "emb_three")
+        gate_last = load(gate[2], [P, V], "gate_last")
         w2_codes = sb.tile([P, 2 * N], U8, name="w2_codes", align_bytes=64)
         nc.sync.dma_start(w2_codes[:], w2_words[0])
         w2_scale = sb.tile([P, N], U8, name="w2_scale", align_bytes=64)
@@ -66,27 +82,49 @@ def tile_picked_devox_none_e_kernel(
                 w2_scales[0, 4 * q : 4 * q + 4, :].bitcast(I32),
             )
         pos_sb = [load_list(src, f"pos{d}_sb") for d, src in enumerate((pos1, pos2, pos3))]
+        gate_cols = [sb.tile([P, BLOCKS], F32, name=f"gate_cols{d}") for d in range(2)]
+        for d in range(2):
+            with nc.allow_non_contiguous_dma(reason="one gate value to a partition"):
+                nc.sync.dma_start(gate_cols[d][:], gate[d, 0, :].rearrange("(b p) -> p b", p=P))
 
-        ident32 = sb.tile([P, P], F32, name="ident32")
-        make_identity(nc, ident32[:])
-        ident16 = sb.tile([P, P], BF16, name="ident16")
-        make_identity(nc, ident16[:])
+        ident = sb.tile([P, P], F32, name="ident")
+        make_identity(nc, ident[:])
+        zT_two = [sb.tile([P, BLOCKS, P, 2], BF16, name=f"zT_two{a}", tag=f"zT_two{a}") for a in range(2)]
 
-        up = [sb.tile([P, U], F32, name=f"up{t}") for t in range(PACK)]
-        for t in range(PACK):
-            nc.vector.memset(up[t][:], 0.0)
+        up = [sb.tile([P, U], F32, name=f"up{s}") for s in range(PACK)]
+        for s in range(PACK):
+            nc.vector.memset(up[s][:], 0.0)
+        zT_two_words = [zT_two[a][:].rearrange("p b c e -> p b (c e)").bitcast(F32) for a in range(2)]
+        for a in range(2):
+            nc.vector.memset(zT_two_words[a], 1.0)
 
-        w1_grouped = sb.tile([P, PACK * H], BF16, name="w1_grouped", align_bytes=64)
-        nc.scalar.activation(
-            w1_grouped[:].rearrange("p (t m j) -> p m j t", t=PACK, j=PACK),
-            w1_raw[:].rearrange("p j (m t) -> p m j t", t=PACK),
-            COPY,
-        )
+        w1_first = sb.tile([P, P, PACK], BF16, name="w1_first", align_bytes=64)
+        w1_rest = sb.tile([P, 3, P, PACK], BF16, name="w1_rest", align_bytes=64)
         w1_codes = sb.tile([P, H], U32, name="w1_codes", align_bytes=64)
         w1_scale = sb.tile([P, H], U8, name="w1_scale", align_bytes=64)
-        nc.vector.quantize_mx(out=w1_codes[:].bitcast(FP8X4), scales=w1_scale[:], in_=w1_grouped[:])
 
-        x_grouped = [sb.tile([P, HALF, PACK], BF16, name=f"x_grouped{a}", align_bytes=64) for a in range(2)]
+        def group_pairs(dst, raw):
+            nc.scalar.activation(
+                dst.rearrange("p (m e) j -> p m j e", e=2),
+                raw[:].rearrange("p j (m t) -> p m j t", t=PACK)[:, :, :, 0:2],
+                COPY,
+            )
+
+        def group_singles(h, raw):
+            nc.scalar.activation(
+                w1_rest[:, 1:3, 64 * h : 64 * (h + 1), :].rearrange("p s m j -> p m j s"),
+                raw[:].rearrange("p j (m t) -> p m j t", t=PACK)[:, :, :, 2:4],
+                COPY,
+            )
+
+        def quantize(codes, scale, cols, values):
+            nc.vector.quantize_mx(out=codes[:, cols].bitcast(FP8X4), scales=scale[:, cols], in_=values)
+
+        group_pairs(w1_first[:], w1_low)
+        group_singles(0, w1_low)
+        quantize(w1_codes, w1_scale, slice(0, P), w1_first[:].rearrange("p c j -> p (c j)"))
+
+        x_grouped = sb.tile([P, S, PACK], BF16, name="x_grouped", align_bytes=64)
         x_codes = sb.tile([P, S], U32, name="x_codes", align_bytes=64)
         x_scale = sb.tile([P, S], U8, name="x_scale", align_bytes=64)
 
@@ -97,139 +135,135 @@ def tile_picked_devox_none_e_kernel(
             return tile[:, a * HALF // LIST : (a + 1) * HALF // LIST]
 
         for j in range(PACK):
-            for a in range(2):
-                nc.vector.tensor_copy(x_grouped[a][:, :, j], x_plane[j][:].indirect(half_list(offs_sb, a)))
-                if j == PACK - 1:
-                    nc.vector.quantize_mx(
-                        out=x_codes[:, half_cols(a)].bitcast(FP8X4),
-                        scales=x_scale[:, half_cols(a)],
-                        in_=x_grouped[a][:].rearrange("p c j -> p (c j)"),
-                    )
+            nc.vector.tensor_copy(x_grouped[:, :, j], x_plane[j][:].indirect(offs_sb[:]))
+        quantize(x_codes, x_scale, slice(0, S), x_grouped[:].rearrange("p c j -> p (c j)"))
 
-        def first_product(t, cols, bank_index, name):
+        group_singles(1, w1_high)
+        quantize(w1_codes, w1_scale, slice(3 * P, 4 * P), w1_rest[:, 2].rearrange("p c j -> p (c j)"))
+
+        def product(acc, lhsT, lhsT_scale, rhs, rhs_scale):
+            nc.tensor.matmul_mx(out=acc, lhsT=lhsT, lhsT_scale=lhsT_scale, rhs=rhs, rhs_scale=rhs_scale,
+                                start=True, stop=True)
+
+        def first_product(s, cols, bank_index, name, tag):
             width = cols.stop - cols.start
             acc = bank(bank_index, [P, width], F32, f"h_acc{name}")
-            m_cols = slice(t * P, (t + 1) * P)
-            nc.tensor.matmul_mx(
-                out=acc[:],
-                lhsT=w1_codes[:, m_cols].bitcast(FP8X4),
-                lhsT_scale=w1_scale[:, m_cols],
-                rhs=x_codes[:, cols].bitcast(FP8X4),
-                rhs_scale=x_scale[:, cols],
-                start=True,
-                stop=True,
-            )
-            h = sb.tile([P, width], F32, name=f"h{name}")
+            m_cols = slice(s * P, (s + 1) * P)
+            product(acc[:], w1_codes[:, m_cols].bitcast(FP8X4), w1_scale[:, m_cols],
+                    x_codes[:, cols].bitcast(FP8X4), x_scale[:, cols])
+            h = sb.tile([P, width], F32, name=f"h{name}", tag=tag)
             nc.scalar.activation(h[:], acc[:], RELU)
             return h
 
-        h_first = [first_product(0, half_cols(a), a, f"0_{a}") for a in range(2)]
-        h_rest = [first_product(t, slice(0, S), t + 1, f"{t}") for t in range(1, PACK)]
+        h_first = [first_product(0, half_cols(0), 0, "low_0", "h_low")]
+        group_pairs(w1_rest[:, 0], w1_high)
+        quantize(w1_codes, w1_scale, slice(P, 3 * P), w1_rest[:, 0:2].rearrange("p s c j -> p (s c j)"))
+        h_first.append(first_product(0, half_cols(1), 1, "low_1", "w1_high"))
+        h_rest = [first_product(s, slice(0, S), index, f"{s}", f"h{s}") for s, index in ((2, 2), (1, 3), (3, 2))]
 
-        z_planes = [sb.tile([P, PACK, PIECE], BF16, name=f"z_planes{q}", align_bytes=64) for q in range(U // PIECE)]
+        z_words = [sb.tile([P, 2, PIECE], F32, name=f"z_words{q}", tag=f"z_words{q}") for q in range(U // PIECE)]
+        zT_pairs = [sb.tile([P, BLOCKS, 2 * P], BF16, name=f"zT_pairs{a}") for a in range(2)]
 
-        def open_sum(t, banks):
+        def open_sums(emb_tile, banks, name):
             sums = []
             for a in range(2):
-                acc = bank(banks[a], [P, 4, P], F32, f"zT_acc{t}_{a}")
-                for b in range(4):
-                    c0 = (4 * a + b) * P
-                    nc.tensor.matmul(acc[:, b, :], emb_plane[t][:, c0 : c0 + P], ident32[:],
+                acc = bank(banks[a], [P, BLOCKS, P], F32, f"zT_acc{name}_{a}")
+                for b in range(BLOCKS):
+                    c0 = (BLOCKS * a + b) * P
+                    nc.tensor.matmul(acc[:, b, :], emb_tile[:, c0 : c0 + P], ident[:],
                                      start=(b == 0), stop=False, is_transpose=True)
                 sums.append(acc)
             return sums
 
-        def close_sum(t, sums, banks):
-            turned = []
+        def close_sums(sums, window, targets, identity):
             for a in range(2):
-                for b in range(4):
-                    c0 = (4 * a + b) * P
-                    nc.tensor.matmul(sums[a][:, b, :], up[t][:, c0 : c0 + P], ident32[:],
-                                     start=False, stop=(b == 3), is_transpose=True)
-                zT = sb.tile([P, 4, P], BF16, name=f"zT{t}_{a}")
-                nc.scalar.copy(zT[:], sums[a][:])
-                turned.append(zT)
-            for a in range(2):
-                back = bank(banks[a], [P, 4, P], BF16, f"z_back{t}_{a}")
-                for b in range(4):
-                    nc.tensor.transpose(back[:, b, :], turned[a][:, b, :], ident16[:])
-                for e in range(2):
-                    nc.scalar.copy(
-                        z_planes[2 * a + e][:, t, :],
-                        back[:, 2 * e : 2 * e + 2, :].rearrange("p b c -> p (b c)"),
-                    )
+                for b in range(BLOCKS):
+                    c0 = (BLOCKS * a + b) * P
+                    nc.tensor.matmul(sums[a][:, b, :], window[:, c0 : c0 + P], identity[:],
+                                     start=False, stop=(b == BLOCKS - 1), is_transpose=True)
+                nc.scalar.copy(targets[a], sums[a][:])
 
-        sum_banks = [(5, 6), (1, 2), (5, 6)]
-        back_banks = [(7, 0), (3, 4), (7, 0)]
-        for t in range(PACK):
-            if t < PACK - 1:
-                sums = open_sum(t, sum_banks[t])
-            if t == 0:
-                for a in range(2):
-                    nc.vector.tensor_copy(up[0][:].indirect(half_list(cell_sb, a)), h_first[a][:])
-            else:
-                nc.vector.tensor_copy(up[t][:].indirect(cell_sb[:]), h_rest[t - 1][:])
-            if t < PACK - 1:
-                close_sum(t, sums, back_banks[t])
+        def turn_back(words, bank_index, name):
+            back = bank(bank_index, [P, BLOCKS, P], F32, name)
+            for b in range(BLOCKS):
+                nc.tensor.transpose(back[:, b, :], words[:, b, :], ident[:])
+            return back
 
-        gate_cols = sb.tile([P, 2, 4], F32, name="gate_cols")
-        for d in range(2):
-            turned = bank(1 + d, [P, 4, P], F32, f"gate_turned{d}")
-            for b in range(4):
-                nc.tensor.transpose(turned[:, b, :], gate_sb[d][:, b * P : (b + 1) * P], ident32[:])
-            nc.scalar.copy(gate_cols[:, d, :], turned[:, :, 0])
-
-        y = [sb.tile([P, U], F32, name=f"y{m}") for m in range(2)]
-        last = PACK - 1
-        for q in range(U // PIECE):
-            cols = slice(q * PIECE, (q + 1) * PIECE)
-            nc.vector.tensor_tensor(z_planes[q][:, last, :], up[last][:, cols], emb_plane[last][:, cols], ADD)
-        z_grouped = [sb.tile([P, PIECE, PACK], BF16, name=f"z_grouped{q}", align_bytes=64) for q in range(U // PIECE)]
-        for q in (0, 2, 1, 3):
-            dst = z_grouped[q][:].rearrange("p (c i) t -> p c t i", i=4)
-            src = z_planes[q][:].rearrange("p t (c i) -> p c t i", i=4)
-            if q % 2 == 0:
-                nc.scalar.copy(dst, src)
-            else:
-                nc.vector.tensor_copy(dst, src)
-        for step, q in enumerate((1, 0, 3, 2)):
-            cols = slice(q * PIECE, (q + 1) * PIECE)
-            z_codes = sb.tile([P, PIECE], U32, name=f"z_codes{q}", align_bytes=64)
-            z_scale = sb.tile([P, PIECE], U8, name=f"z_scale{q}", align_bytes=64)
-            nc.vector.quantize_mx(out=z_codes[:].bitcast(FP8X4), scales=z_scale[:],
-                                  in_=z_grouped[q][:].rearrange("p c t -> p (c t)"))
-            for m in range(2):
-                acc = bank((1 + 2 * step + m) % 8, [P, PIECE], F32, f"y_acc{q}_{m}")
-                nc.tensor.matmul_mx(
-                    out=acc[:],
-                    lhsT=w2_codes[:, 2 * P * m : 2 * P * (m + 1)].bitcast(FP4X4),
-                    lhsT_scale=w2_scale[:, P * m : P * (m + 1)],
-                    rhs=z_codes[:].bitcast(FP8X4),
-                    rhs_scale=z_scale[:],
-                    start=True,
-                    stop=True,
+        def copy_back(back, a, u):
+            for e in range(2):
+                nc.scalar.copy(
+                    z_words[2 * a + e][:, u, :],
+                    back[:, 2 * e : 2 * e + 2, :].rearrange("p b c -> p (b c)"),
                 )
-                nc.scalar.copy(y[m][:, cols], acc[:])
+
+        sums_low = open_sums(emb_low, (5, 6), "low")
+        sums_two = open_sums(emb_two, (7, 4), "two")
+        sums_high = open_sums(emb_high, (0, 1), "high")
+        for a in range(2):
+            nc.vector.tensor_copy(up[0][:].indirect(half_list(cell_sb, a)), h_first[a][:])
+        close_sums(sums_low, up[0], [zT_pairs[a][:, :, 0:P] for a in range(2)], ident)
+        nc.vector.tensor_copy(up[1][:].indirect(cell_sb[:]), h_rest[0][:])
+        close_sums(sums_two, up[1], [zT_two[a][:, :, :, 0] for a in range(2)], ident)
+        copy_back(turn_back(zT_two_words[0], 2, "two_back0"), 0, 1)
+        back = turn_back(zT_two_words[1], 3, "two_back1")
+        ident_late = sb.tile([P, P], F32, name="ident_late", tag="zT_two1")
+        nc.scalar.copy(ident_late[:], ident[:])
+        copy_back(back, 1, 1)
+        nc.vector.tensor_copy(up[2][:].indirect(cell_sb[:]), h_rest[1][:])
+        close_sums(sums_high, up[2], [zT_pairs[a][:, :, P : 2 * P] for a in range(2)], ident_late)
+        for a in range(2):
+            copy_back(turn_back(zT_pairs[a][:].bitcast(F32), 5 + a, f"pairs_back{a}"), a, 0)
+        nc.vector.tensor_copy(up[3][:].indirect(cell_sb[:]), h_rest[2][:])
+
+        pieces = range(U // PIECE)
+        piece_cols = [slice(q * PIECE, (q + 1) * PIECE) for q in pieces]
+        for q in pieces:
+            odd = z_words[q][:, 1, :].bitcast(BF16).rearrange("p (c e) -> p c e", e=2)[:, :, 1]
+            nc.vector.tensor_tensor(odd, up[3][:, piece_cols[q]], emb_three[:, piece_cols[q]], ADD)
+        z_grouped = [sb.tile([P, PIECE, 2], F32, name=f"z_grouped{q}", align_bytes=64) for q in pieces]
+        for q in pieces:
+            weave = nc.vector.tensor_copy if q == pieces[-1] else nc.scalar.copy
+            weave(
+                z_grouped[q][:].rearrange("p (c i) u -> p c u i", i=4),
+                z_words[q][:].rearrange("p u (c i) -> p c u i", i=4),
+            )
+        y = [sb.tile([P, U], F32, name="y0", tag="z_words2"), sb.tile([P, U], F32, name="y1")]
+        z_codes = sb.tile([P, U], U32, name="z_codes", align_bytes=64)
+        z_scale = sb.tile([P, U], U8, name="z_scale", align_bytes=64)
+
+        def second_product(m, cols, bank_index):
+            acc = bank(bank_index, [P, cols.stop - cols.start], F32, f"y_acc{m}_{cols.start}")
+            product(acc[:], w2_codes[:, 2 * P * m : 2 * P * (m + 1)].bitcast(FP4X4), w2_scale[:, P * m : P * (m + 1)],
+                    z_codes[:, cols].bitcast(FP8X4), z_scale[:, cols])
+            nc.scalar.copy(y[m][:, cols], acc[:])
+
+        for q in pieces:
+            quantize(z_codes, z_scale, piece_cols[q], z_grouped[q][:].rearrange("p c u -> p (c u)").bitcast(BF16))
+            second_product(0, piece_cols[q], (7, 4, 0, 1)[q])
+        for a in range(2):
+            second_product(1, slice(a * U // 2, (a + 1) * U // 2), (4, 1)[a])
 
         partial = []
         for m in range(2):
-            acc = bank(5 + m, [P, 4, P], F32, f"out_acc{m}")
+            acc = bank(2 + m, [P, BLOCKS, P], F32, f"out_acc{m}")
             for d in range(2):
                 picked = sb.tile([P, V], F32, name=f"picked{m}_{d}")
                 nc.vector.tensor_copy(picked[:], y[m][:].indirect(pos_sb[d][:]))
-                turned = bank(1 + 2 * m + d, [P, 4, P], F32, f"picked_turned{m}_{d}")
-                for b in range(4):
-                    nc.tensor.transpose(turned[:, b, :], picked[:, b * P : (b + 1) * P], ident32[:])
-                scaled = sb.tile([P, 4, P], F32, name=f"scaled{m}_{d}")
-                for b in range(4):
-                    nc.scalar.activation(scaled[:, b, :], turned[:, b, :], COPY, scale=gate_cols[:, d, b : b + 1])
-                for b in range(4):
-                    nc.tensor.matmul(acc[:, b, :], scaled[:, b, :], ident32[:],
-                                     start=(d == 0 and b == 0), stop=(d == 1 and b == 3), is_transpose=True)
+                turned = bank((7, 0)[d], [P, BLOCKS, P], F32, f"picked_turned{m}_{d}")
+                for b in range(BLOCKS):
+                    nc.tensor.transpose(turned[:, b, :], picked[:, b * P : (b + 1) * P], ident[:])
+                scaled = sb.tile([P, BLOCKS, P], F32, name=f"scaled{m}_{d}")
+                for b in range(BLOCKS):
+                    nc.scalar.activation(scaled[:, b, :], turned[:, b, :], COPY, scale=gate_cols[d][:, b : b + 1])
+                for b in range(BLOCKS):
+                    nc.tensor.matmul(acc[:, b, :], scaled[:, b, :], ident[:],
+                                     start=(d == 0 and b == 0), stop=(d == 1 and b == BLOCKS - 1), is_transpose=True)
             partial.append(acc)
         for m in range(2):
             third = sb.tile([P, V], F32, name=f"third{m}")
-            nc.vector.tensor_tensor(third[:], y[m][:].indirect(pos_sb[2][:]), gate_sb[2][:], MULT)
-            result = sb.tile([P, V], F32, name=f"result{m}")
-            nc.vector.tensor_tensor(result[:], partial[m][:].rearrange("p b c -> p (b c)"), third[:], ADD)
-            nc.sync.dma_start(out[m * P : (m + 1) * P, :], result[:])
+            nc.vector.tensor_tensor(third[:], y[m][:].indirect(pos_sb[2][:]), gate_last[:], MULT)
+            summed = partial[m][:].rearrange("p b c -> p (b c)")
+            for cols in ([slice(0, V)] if m == 0 else [half_cols(0), half_cols(1)]):
+                result = sb.tile([P, cols.stop - cols.start], F32, name=f"result{m}_{cols.start}")
+                nc.vector.tensor_tensor(result[:], summed[:, cols], third[:, cols], ADD)
+                nc.sync.dma_start(out[m * P : (m + 1) * P, cols], result[:])

@@ -98,7 +98,7 @@ def tile_picked_devox_none_e_kernel(
         for a in range(2):
             nc.vector.memset(zT_two_words[a], 1.0)
 
-        w1_first = sb.tile([P, P, PACK], BF16, name="w1_first", align_bytes=64)
+        w1_first = sb.tile([P, P, PACK], BF16, name="w1_first", tag="w1_first", align_bytes=64)
         w1_rest = sb.tile([P, 3, P, PACK], BF16, name="w1_rest", align_bytes=64)
         w1_codes = sb.tile([P, H], U32, name="w1_codes", align_bytes=64)
         w1_scale = sb.tile([P, H], U8, name="w1_scale", align_bytes=64)
@@ -125,8 +125,9 @@ def tile_picked_devox_none_e_kernel(
         quantize(w1_codes, w1_scale, slice(0, P), w1_first[:].rearrange("p c j -> p (c j)"))
 
         x_grouped = sb.tile([P, S, PACK], BF16, name="x_grouped", align_bytes=64)
-        x_codes = sb.tile([P, S], U32, name="x_codes", align_bytes=64)
-        x_scale = sb.tile([P, S], U8, name="x_scale", align_bytes=64)
+        x_codes = [sb.tile([P, HALF], U32, name="x_codes0", align_bytes=64),
+                   sb.tile([P, HALF], U32, name="x_codes1", tag="w1_first", align_bytes=64)]
+        x_scale = [sb.tile([P, HALF], U8, name=f"x_scale{a}", align_bytes=64) for a in range(2)]
 
         def half_cols(a):
             return slice(a * HALF, (a + 1) * HALF)
@@ -136,7 +137,8 @@ def tile_picked_devox_none_e_kernel(
 
         for j in range(PACK):
             nc.vector.tensor_copy(x_grouped[:, :, j], x_plane[j][:].indirect(offs_sb[:]))
-        quantize(x_codes, x_scale, slice(0, S), x_grouped[:].rearrange("p c j -> p (c j)"))
+        for a in range(2):
+            quantize(x_codes[a], x_scale[a], slice(0, HALF), x_grouped[:, half_cols(a), :].rearrange("p c j -> p (c j)"))
 
         group_singles(1, w1_high)
         quantize(w1_codes, w1_scale, slice(3 * P, 4 * P), w1_rest[:, 2].rearrange("p c j -> p (c j)"))
@@ -145,21 +147,22 @@ def tile_picked_devox_none_e_kernel(
             nc.tensor.matmul_mx(out=acc, lhsT=lhsT, lhsT_scale=lhsT_scale, rhs=rhs, rhs_scale=rhs_scale,
                                 start=True, stop=True)
 
-        def first_product(s, cols, bank_index, name, tag):
-            width = cols.stop - cols.start
+        def first_product(s, halves, bank_index, name, tag):
+            width = HALF * len(halves)
             acc = bank(bank_index, [P, width], F32, f"h_acc{name}")
             m_cols = slice(s * P, (s + 1) * P)
-            product(acc[:], w1_codes[:, m_cols].bitcast(FP8X4), w1_scale[:, m_cols],
-                    x_codes[:, cols].bitcast(FP8X4), x_scale[:, cols])
+            for n, a in enumerate(halves):
+                product(acc[:, half_cols(n)], w1_codes[:, m_cols].bitcast(FP8X4), w1_scale[:, m_cols],
+                        x_codes[a][:].bitcast(FP8X4), x_scale[a][:])
             h = sb.tile([P, width], F32, name=f"h{name}", tag=tag)
             nc.scalar.activation(h[:], acc[:], RELU)
             return h
 
-        h_first = [first_product(0, half_cols(0), 0, "low_0", "h_low")]
+        h_first = [first_product(0, [0], 0, "low_0", "h_low")]
         group_pairs(w1_rest[:, 0], w1_high)
         quantize(w1_codes, w1_scale, slice(P, 3 * P), w1_rest[:, 0:2].rearrange("p s c j -> p (s c j)"))
-        h_first.append(first_product(0, half_cols(1), 1, "low_1", "w1_high"))
-        h_rest = [first_product(s, slice(0, S), index, f"{s}", f"h{s}") for s, index in ((2, 2), (1, 3), (3, 2))]
+        h_first.append(first_product(0, [1], 1, "low_1", "w1_high"))
+        h_rest = [first_product(s, [0, 1], index, f"{s}", f"h{s}") for s, index in ((2, 2), (1, 3), (3, 2))]
 
         z_words = [sb.tile([P, 2, PIECE], F32, name=f"z_words{q}", tag=f"z_words{q}") for q in range(U // PIECE)]
         zT_pairs = [sb.tile([P, BLOCKS, 2 * P], BF16, name=f"zT_pairs{a}") for a in range(2)]
@@ -247,7 +250,7 @@ def tile_picked_devox_none_e_kernel(
         for m in range(2):
             acc = bank(2 + m, [P, BLOCKS, P], F32, f"out_acc{m}")
             for d in range(2):
-                picked = sb.tile([P, V], F32, name=f"picked{m}_{d}")
+                picked = sb.tile([P, V], F32, name=f"picked{m}_{d}", tag=f"picked{m}_{d}")
                 nc.vector.tensor_copy(picked[:], y[m][:].indirect(pos_sb[d][:]))
                 turned = bank((7, 0)[d], [P, BLOCKS, P], F32, f"picked_turned{m}_{d}")
                 for b in range(BLOCKS):
@@ -260,7 +263,7 @@ def tile_picked_devox_none_e_kernel(
                                      start=(d == 0 and b == 0), stop=(d == 1 and b == BLOCKS - 1), is_transpose=True)
             partial.append(acc)
         for m in range(2):
-            third = sb.tile([P, V], F32, name=f"third{m}")
+            third = sb.tile([P, V], F32, name=f"third{m}", tag=("picked0_1", "third1")[m])
             nc.vector.tensor_tensor(third[:], y[m][:].indirect(pos_sb[2][:]), gate_last[:], MULT)
             summed = partial[m][:].rearrange("p b c -> p (b c)")
             for cols in ([slice(0, V)] if m == 0 else [half_cols(0), half_cols(1)]):

from contextlib import ExitStack

import concourse.mybir as mybir
from concourse.masks import make_identity

K, T, S, V, H, N, U = 512, 2048, 512, 512, 512, 256, 1024
FLOPS = 2 * K * H * S + 2 * H * N * U

F32 = mybir.dt.float32
BF16 = mybir.dt.bfloat16
I32 = mybir.dt.int32
U32 = mybir.dt.uint32
U16 = mybir.dt.uint16
U8 = mybir.dt.uint8
FP8X4 = mybir.dt.float8_e4m3fn_x4
FP4X4 = mybir.dt.float4_e2m1fn_x4
ADD = mybir.AluOpType.add
MULT = mybir.AluOpType.mult
COPY = mybir.ActivationFunctionType.Copy
RELU = mybir.ActivationFunctionType.Relu

P = 128
PACK = 4
HALF = S // 2
PIECE = 256
LIST = 16
BLOCKS = 4


def tile_picked_devox_none_e_kernel(
    tc, xT, w1, w2_words, w2_scales, gate, emb, offs, cell, pos1, pos2, pos3, out
):
    nc = tc.nc
    with ExitStack() as ctx:
        lists = ctx.enter_context(tc.tile_pool(name="lists", bufs=1))
        sb = ctx.enter_context(tc.tile_pool(name="sb", bufs=1))
        psum = ctx.enter_context(tc.psum_pool(name="psum", bufs=1))

        def bank(index, shape, dtype, name):
            return psum.tile(shape, dtype, name=name, tag=f"bank{index}")

        def load_list(source, name):
            tile = lists.tile([P, S // LIST], U16, name=name)
            nc.sync.dma_start(tile[:], source)
            return tile

        def load(source, shape, name):
            tile = sb.tile(shape, F32, name=name)
            nc.sync.dma_start(tile[:], source)
            return tile

        def load_emb_rows(tile, h, e):
            rows = emb.rearrange("(h m t) r -> h t m r", h=2, t=PACK)
            nc.sync.dma_start(tile[e:P:2, :], rows[h][e])

        w1_halves = w1.rearrange("(p j) (h c) -> h p j c", j=PACK, h=2)
        x_rows = xT.rearrange("(p j) c -> j p c", j=PACK)
        emb_rows = emb.rearrange("(p j) r -> j p r", j=PACK)
        x_plane = [load(x_rows[0], [P, T], "x_plane0")]
        offs_sb = load_list(offs, "offs_sb")
        x_plane.extend(load(x_rows[j], [P, T], f"x_plane{j}") for j in range(1, PACK))
        w1_low = load(w1_halves[0], [P, PACK, H // 2], "w1_low")
        cell_sb = load_list(cell, "cell_sb")
        emb_low = sb.tile([P, U], F32, name="emb_low")
        load_emb_rows(emb_low, 0, 0)
        w1_high = sb.tile([P, PACK, H // 2], F32, name="w1_high", tag="w1_high")
        nc.sync.dma_start(w1_high[:], w1_halves[1])
        load_emb_rows(emb_low, 0, 1)
        emb_two = load(emb_rows[2], [P, U], "emb_two")
        emb_high = sb.tile([P, U], F32, name="emb_high")
        for e in range(2):
            load_emb_rows(emb_high, 1, e)
        emb_three = load(emb_rows[3], [P, U], "emb_three")
        gate_last = load(gate[2], [P, V], "gate_last")
        w2_codes = sb.tile([P, 2 * N], U8, name="w2_codes", align_bytes=64)
        nc.sync.dma_start(w2_codes[:], w2_words[0])
        w2_scale = sb.tile([P, N], U8, name="w2_scale", align_bytes=64)
        nc.vector.memset(w2_scale[:].bitcast(I32), 0)
        for q in range(4):
            nc.sync.dma_start(
                w2_scale[32 * q : 32 * q + 4, :].bitcast(I32),
                w2_scales[0, 4 * q : 4 * q + 4, :].bitcast(I32),
            )
        pos_sb = [load_list(src, f"pos{d}_sb") for d, src in enumerate((pos1, pos2, pos3))]
        gate_cols = [sb.tile([P, BLOCKS], F32, name=f"gate_cols{d}") for d in range(2)]
        for d in range(2):
            with nc.allow_non_contiguous_dma(reason="one gate value to a partition"):
                nc.sync.dma_start(gate_cols[d][:], gate[d, 0, :].rearrange("(b p) -> p b", p=P))

        ident = sb.tile([P, P], F32, name="ident")
        make_identity(nc, ident[:])
        zT_two = [sb.tile([P, BLOCKS, P, 2], BF16, name=f"zT_two{a}", tag=f"zT_two{a}") for a in range(2)]

        up = [sb.tile([P, U], F32, name=f"up{s}") for s in range(PACK)]
        for s in range(PACK):
            nc.vector.memset(up[s][:], 0.0)
        zT_two_words = [zT_two[a][:].rearrange("p b c e -> p b (c e)").bitcast(F32) for a in range(2)]
        for a in range(2):
            nc.vector.memset(zT_two_words[a], 1.0)

        w1_first = sb.tile([P, P, PACK], BF16, name="w1_first", tag="w1_first", align_bytes=64)
        w1_rest = sb.tile([P, 3, P, PACK], BF16, name="w1_rest", align_bytes=64)
        w1_codes = sb.tile([P, H], U32, name="w1_codes", align_bytes=64)
        w1_scale = sb.tile([P, H], U8, name="w1_scale", align_bytes=64)

        def group_pairs(dst, raw):
            nc.scalar.activation(
                dst.rearrange("p (m e) j -> p m j e", e=2),
                raw[:].rearrange("p j (m t) -> p m j t", t=PACK)[:, :, :, 0:2],
                COPY,
            )

        def group_singles(h, raw):
            nc.scalar.activation(
                w1_rest[:, 1:3, 64 * h : 64 * (h + 1), :].rearrange("p s m j -> p m j s"),
                raw[:].rearrange("p j (m t) -> p m j t", t=PACK)[:, :, :, 2:4],
                COPY,
            )

        def quantize(codes, scale, cols, values):
            nc.vector.quantize_mx(out=codes[:, cols].bitcast(FP8X4), scales=scale[:, cols], in_=values)

        group_pairs(w1_first[:], w1_low)
        group_singles(0, w1_low)
        quantize(w1_codes, w1_scale, slice(0, P), w1_first[:].rearrange("p c j -> p (c j)"))

        x_grouped = sb.tile([P, S, PACK], BF16, name="x_grouped", align_bytes=64)
        x_codes = [sb.tile([P, HALF], U32, name="x_codes0", align_bytes=64),
                   sb.tile([P, HALF], U32, name="x_codes1", tag="w1_first", align_bytes=64)]
        x_scale = [sb.tile([P, HALF], U8, name=f"x_scale{a}", align_bytes=64) for a in range(2)]

        def half_cols(a):
            return slice(a * HALF, (a + 1) * HALF)

        def half_list(tile, a):
            return tile[:, a * HALF // LIST : (a + 1) * HALF // LIST]

        for j in range(PACK):
            nc.vector.tensor_copy(x_grouped[:, :, j], x_plane[j][:].indirect(offs_sb[:]))
        for a in range(2):
            quantize(x_codes[a], x_scale[a], slice(0, HALF), x_grouped[:, half_cols(a), :].rearrange("p c j -> p (c j)"))

        group_singles(1, w1_high)
        quantize(w1_codes, w1_scale, slice(3 * P, 4 * P), w1_rest[:, 2].rearrange("p c j -> p (c j)"))

        def product(acc, lhsT, lhsT_scale, rhs, rhs_scale):
            nc.tensor.matmul_mx(out=acc, lhsT=lhsT, lhsT_scale=lhsT_scale, rhs=rhs, rhs_scale=rhs_scale,
                                start=True, stop=True)

        def first_product(s, halves, bank_index, name, tag):
            width = HALF * len(halves)
            acc = bank(bank_index, [P, width], F32, f"h_acc{name}")
            m_cols = slice(s * P, (s + 1) * P)
            for n, a in enumerate(halves):
                product(acc[:, half_cols(n)], w1_codes[:, m_cols].bitcast(FP8X4), w1_scale[:, m_cols],
                        x_codes[a][:].bitcast(FP8X4), x_scale[a][:])
            h = sb.tile([P, width], F32, name=f"h{name}", tag=tag)
            nc.scalar.activation(h[:], acc[:], RELU)
            return h

        h_first = [first_product(0, [0], 0, "low_0", "h_low")]
        group_pairs(w1_rest[:, 0], w1_high)
        quantize(w1_codes, w1_scale, slice(P, 3 * P), w1_rest[:, 0:2].rearrange("p s c j -> p (s c j)"))
        h_first.append(first_product(0, [1], 1, "low_1", "w1_high"))
        h_rest = [first_product(s, [0, 1], index, f"{s}", f"h{s}") for s, index in ((2, 2), (1, 3), (3, 2))]

        z_words = [sb.tile([P, 2, PIECE], F32, name=f"z_words{q}", tag=f"z_words{q}") for q in range(U // PIECE)]
        zT_pairs = [sb.tile([P, BLOCKS, 2 * P], BF16, name=f"zT_pairs{a}") for a in range(2)]

        def open_sums(emb_tile, banks, name):
            sums = []
            for a in range(2):
                acc = bank(banks[a], [P, BLOCKS, P], F32, f"zT_acc{name}_{a}")
                for b in range(BLOCKS):
                    c0 = (BLOCKS * a + b) * P
                    nc.tensor.matmul(acc[:, b, :], emb_tile[:, c0 : c0 + P], ident[:],
                                     start=(b == 0), stop=False, is_transpose=True)
                sums.append(acc)
            return sums

        def close_sums(sums, window, targets, identity):
            for a in range(2):
                for b in range(BLOCKS):
                    c0 = (BLOCKS * a + b) * P
                    nc.tensor.matmul(sums[a][:, b, :], window[:, c0 : c0 + P], identity[:],
                                     start=False, stop=(b == BLOCKS - 1), is_transpose=True)
                nc.scalar.copy(targets[a], sums[a][:])

        def turn_back(words, bank_index, name):
            back = bank(bank_index, [P, BLOCKS, P], F32, name)
            for b in range(BLOCKS):
                nc.tensor.transpose(back[:, b, :], words[:, b, :], ident[:])
            return back

        def copy_back(back, a, u):
            for e in range(2):
                nc.scalar.copy(
                    z_words[2 * a + e][:, u, :],
                    back[:, 2 * e : 2 * e + 2, :].rearrange("p b c -> p (b c)"),
                )

        sums_low = open_sums(emb_low, (5, 6), "low")
        sums_two = open_sums(emb_two, (7, 4), "two")
        sums_high = open_sums(emb_high, (0, 1), "high")
        for a in range(2):
            nc.vector.tensor_copy(up[0][:].indirect(half_list(cell_sb, a)), h_first[a][:])
        close_sums(sums_low, up[0], [zT_pairs[a][:, :, 0:P] for a in range(2)], ident)
        nc.vector.tensor_copy(up[1][:].indirect(cell_sb[:]), h_rest[0][:])
        close_sums(sums_two, up[1], [zT_two[a][:, :, :, 0] for a in range(2)], ident)
        copy_back(turn_back(zT_two_words[0], 2, "two_back0"), 0, 1)
        back = turn_back(zT_two_words[1], 3, "two_back1")
        ident_late = sb.tile([P, P], F32, name="ident_late", tag="zT_two1")
        nc.scalar.copy(ident_late[:], ident[:])
        copy_back(back, 1, 1)
        nc.vector.tensor_copy(up[2][:].indirect(cell_sb[:]), h_rest[1][:])
        close_sums(sums_high, up[2], [zT_pairs[a][:, :, P : 2 * P] for a in range(2)], ident_late)
        for a in range(2):
            copy_back(turn_back(zT_pairs[a][:].bitcast(F32), 5 + a, f"pairs_back{a}"), a, 0)
        nc.vector.tensor_copy(up[3][:].indirect(cell_sb[:]), h_rest[2][:])

        pieces = range(U // PIECE)
        piece_cols = [slice(q * PIECE, (q + 1) * PIECE) for q in pieces]
        for q in pieces:
            odd = z_words[q][:, 1, :].bitcast(BF16).rearrange("p (c e) -> p c e", e=2)[:, :, 1]
            nc.vector.tensor_tensor(odd, up[3][:, piece_cols[q]], emb_three[:, piece_cols[q]], ADD)
        z_grouped = [sb.tile([P, PIECE, 2], F32, name=f"z_grouped{q}", align_bytes=64) for q in pieces]
        for q in pieces:
            weave = nc.vector.tensor_copy if q == pieces[-1] else nc.scalar.copy
            weave(
                z_grouped[q][:].rearrange("p (c i) u -> p c u i", i=4),
                z_words[q][:].rearrange("p u (c i) -> p c u i", i=4),
            )
        y = [sb.tile([P, U], F32, name="y0", tag="z_words2"), sb.tile([P, U], F32, name="y1")]
        z_codes = sb.tile([P, U], U32, name="z_codes", align_bytes=64)
        z_scale = sb.tile([P, U], U8, name="z_scale", align_bytes=64)

        def second_product(m, cols, bank_index):
            acc = bank(bank_index, [P, cols.stop - cols.start], F32, f"y_acc{m}_{cols.start}")
            product(acc[:], w2_codes[:, 2 * P * m : 2 * P * (m + 1)].bitcast(FP4X4), w2_scale[:, P * m : P * (m + 1)],
                    z_codes[:, cols].bitcast(FP8X4), z_scale[:, cols])
            nc.scalar.copy(y[m][:, cols], acc[:])

        for q in pieces:
            quantize(z_codes, z_scale, piece_cols[q], z_grouped[q][:].rearrange("p c u -> p (c u)").bitcast(BF16))
            second_product(0, piece_cols[q], (7, 4, 0, 1)[q])
        for a in range(2):
            second_product(1, slice(a * U // 2, (a + 1) * U // 2), (4, 1)[a])

        partial = []
        for m in range(2):
            acc = bank(2 + m, [P, BLOCKS, P], F32, f"out_acc{m}")
            for d in range(2):
                picked = sb.tile([P, V], F32, name=f"picked{m}_{d}", tag=f"picked{m}_{d}")
                nc.vector.tensor_copy(picked[:], y[m][:].indirect(pos_sb[d][:]))
                turned = bank((7, 0)[d], [P, BLOCKS, P], F32, f"picked_turned{m}_{d}")
                for b in range(BLOCKS):
                    nc.tensor.transpose(turned[:, b, :], picked[:, b * P : (b + 1) * P], ident[:])
                scaled = sb.tile([P, BLOCKS, P], F32, name=f"scaled{m}_{d}")
                for b in range(BLOCKS):
                    nc.scalar.activation(scaled[:, b, :], turned[:, b, :], COPY, scale=gate_cols[d][:, b : b + 1])
                for b in range(BLOCKS):
                    nc.tensor.matmul(acc[:, b, :], scaled[:, b, :], ident[:],
                                     start=(d == 0 and b == 0), stop=(d == 1 and b == BLOCKS - 1), is_transpose=True)
            partial.append(acc)
        for m in range(2):
            third = sb.tile([P, V], F32, name=f"third{m}", tag=("picked0_1", "third1")[m])
            nc.vector.tensor_tensor(third[:], y[m][:].indirect(pos_sb[2][:]), gate_last[:], MULT)
            summed = partial[m][:].rearrange("p b c -> p (b c)")
            for cols in ([slice(0, V)] if m == 0 else [half_cols(0), half_cols(1)]):
                result = sb.tile([P, cols.stop - cols.start], F32, name=f"result{m}_{cols.start}")
                nc.vector.tensor_tensor(result[:], summed[:, cols], third[:, cols], ADD)
                nc.sync.dma_start(out[m * P : (m + 1) * P, cols], result[:])
